import numpy as np
import ml_dtypes


def mxq(x, axis, fmt="e4m3"):
    dtype, down = {"e4m3": (ml_dtypes.float8_e4m3fn, 7), "e5m2": (ml_dtypes.float8_e5m2, 14)}[fmt]
    v = np.moveaxis(np.asarray(x, np.float32).astype(ml_dtypes.bfloat16).astype(np.float64), axis, -1)
    blocks = v.reshape(v.shape[:-1] + (-1, 32))
    amax = np.abs(blocks).max(-1, keepdims=True)
    byte = np.maximum(np.where(amax > 0, np.frexp(amax)[1] - 1 + 127, 0) - down, 1)
    scale = np.exp2(byte - 127.0)
    codes = (blocks / scale).astype(np.float32).astype(dtype).astype(np.float64)
    return np.moveaxis((codes * scale).reshape(v.shape), -1, axis)


WIDE = False


def mx_kscale(k):
    if not WIDE:
        return np.ones(k)
    levels = np.array([30, -30])
    if k % 512:
        return np.exp2(np.random.permutation(np.resize(levels, k // 32))).repeat(32)
    a = np.empty((k // 512, 16))
    for p in range(k // 512):
        a[p, :8] = np.random.permutation(np.resize(levels, 8))
        for g in range(8):
            far = levels[np.abs(levels - a[p, g]) >= 10]
            a[p, g + 8] = far[np.random.randint(len(far))]
    return np.exp2(a.ravel()).repeat(32)


def f64(x):
    return np.asarray(x).astype(np.float64)


def striped(idx):
    return np.tile(np.asarray(idx).reshape(-1, 16).T, (8, 1)).astype(np.uint16)


def unstriped(offs):
    return offs[:16].T.reshape(-1).astype(np.int64)


E2M1 = np.array([0.0, 0.5, 1.0, 1.5, 2.0, 3.0, 4.0, 6.0, -0.0, -0.5, -1.0, -1.5, -2.0, -3.0, -4.0, -6.0])


def pack_weight(w, fmt):
    k, n = w.shape
    w = f64(np.asarray(w, np.float32).astype(ml_dtypes.bfloat16)).reshape(k // 32, 32, n)
    amax = np.abs(w).max(1)
    if fmt in ("e4m3", "e5m2"):
        byte = np.frexp(amax)[1] - 1 + 127 - (7 if fmt == "e4m3" else 14)
    else:
        mant, ex = np.frexp(amax / 6.0)
        byte = np.where(mant > 0.5, ex, ex - 1) + 127
    byte = np.clip(np.where(amax > 0, byte, 1), 1, 254)
    scaled = (w * np.exp2(127.0 - byte)[:, None, :]).reshape(k, n).astype(np.float32)
    by_word = np.ascontiguousarray(scaled.reshape(k // 512, 128, 4, n).transpose(0, 1, 3, 2))
    if fmt in ("e4m3", "e5m2"):
        words = by_word.astype(ml_dtypes.float8_e4m3fn if fmt == "e4m3" else ml_dtypes.float8_e5m2).view(np.uint8)
    else:
        c = by_word.astype(ml_dtypes.float4_e2m1fn).view(np.uint8) & 0xF
        words = (c[..., 0::2] | (c[..., 1::2] << 4)).reshape(k // 512, 128, 2 * n)
    return np.ascontiguousarray(words), np.ascontiguousarray(byte.astype(np.uint8).reshape(k // 512, 16, n))


def unpack_weight(words, scales, fmt):
    g, _, n = scales.shape
    words = np.ascontiguousarray(words).reshape(g, 128, n, -1)
    if fmt in ("e4m3", "e5m2"):
        vals = words.view(ml_dtypes.float8_e4m3fn if fmt == "e4m3" else ml_dtypes.float8_e5m2).astype(np.float64)
    else:
        nib = np.empty((g, 128, n, 4), np.uint8)
        nib[..., 0::2] = words & 0xF
        nib[..., 1::2] = words >> 4
        vals = E2M1[nib]
    vals = vals * np.repeat(np.exp2(scales.astype(np.float64) - 127.0), 8, axis=1)[..., None]
    return vals.transpose(0, 1, 3, 2).reshape(g * 512, n)


def sigmoid(v):
    return 1.0 / (1.0 + np.exp(-v))


K, T, J, R, O, N, E = 512, 2048, 256, 512, 128, 256, 1024


def setup_inputs():
    n = np.random.standard_normal
    idx = np.random.permutation(T)[:J]
    idx2 = np.random.permutation(T)[:J]
    idx3 = np.random.permutation(J)[:O]
    idx4 = np.random.permutation(J)[:O]
    idx5 = np.random.permutation(E)[:O]
    fk = mx_kscale(K)
    fr = mx_kscale(R)
    xtp = pack_weight(n((K, T)) / fk[:, None], "e4m3")
    wp = pack_weight(n((K, R)) * 1 / np.sqrt(K) * fk[:, None], "e2m1")
    w2p = pack_weight(n((K, R)) * 1 / np.sqrt(K) * fk[:, None] * fr, "e5m2")
    wbp = pack_weight(n((R, N)) * 1 / np.sqrt(R) / fr[:, None], "e5m2")
    return {
        "xt_words": xtp[0],
        "xt_scales": xtp[1],
        "w_words": wp[0],
        "w_scales": wp[1],
        "w2_words": w2p[0],
        "w2_scales": w2p[1],
        "sg": (np.random.uniform(0.6, 1.6, (R, 1))).astype(np.float32),
        "bg": (np.random.uniform(-1.0, 1.0, (R, 1))).astype(np.float32),
        "wb_words": wbp[0],
        "wb_scales": wbp[1],
        "tz": (n((N, E))).astype(np.float32),
        "offs": striped(idx),
        "offs2": striped(idx2),
        "offs3": striped(idx3),
        "offs4": striped(idx4),
        "offs5": striped(idx5),
    }


def reference(xt_words, xt_scales, w_words, w_scales, w2_words, w2_scales, sg, bg, wb_words, wb_scales, tz, offs, offs2, offs3, offs4, offs5):
    idx = unstriped(offs)
    idx2 = unstriped(offs2)
    idx3 = unstriped(offs3)
    idx4 = unstriped(offs4)
    idx5 = unstriped(offs5)
    xtu = unpack_weight(xt_words, xt_scales, "e4m3")
    wu = unpack_weight(w_words, w_scales, "e2m1")
    w2u = unpack_weight(w2_words, w2_scales, "e5m2")
    wbu = unpack_weight(wb_words, wb_scales, "e5m2")
    xtidxg = xtu[:, idx]
    a = wu.T @ xtidxg
    xtidx2g = xtu[:, idx2]
    b = w2u.T @ xtidx2g
    hid = b[:, idx4] * sigmoid(a[:, idx3] * f64(sg) + f64(bg))
    hidq = mxq(hid, 0, "e4m3")
    p = wbu.T @ hidq
    y = p + f64(tz)[:, idx5]
    return y

@@ -1,0 +1,159 @@
+from contextlib import ExitStack
+
+import concourse.mybir as mybir
+
+K, T, J, R, O, N, E = 512, 2048, 256, 512, 128, 256, 1024
+FLOPS = 2 * K * R * J * 2 + 2 * R * N * O
+
+F32 = mybir.dt.float32
+BF16 = mybir.dt.bfloat16
+I32 = mybir.dt.int32
+U32 = mybir.dt.uint32
+U16 = mybir.dt.uint16
+U8 = mybir.dt.uint8
+E4M3 = mybir.dt.float8_e4m3fn_x4
+E5M2 = mybir.dt.float8_e5m2_x4
+E2M1 = mybir.dt.float4_e2m1fn_x4
+ACT = mybir.ActivationFunctionType
+ALU = mybir.AluOpType
+P = 128
+
+
+def tile_list_ahead_gatefetch_one_tabled_kernel(
+    tc, xt_words, xt_scales, w_words, w_scales, w2_words, w2_scales, sg, bg,
+    wb_words, wb_scales, tz, offs, offs2, offs3, offs4, offs5, out,
+):
+    nc = tc.nc
+    with ExitStack() as ctx:
+        sb = ctx.enter_context(tc.tile_pool(name="sb", bufs=1))
+        ps = ctx.enter_context(tc.psum_pool(name="ps", bufs=1))
+
+        def tile(name, shape, dtype):
+            return sb.tile(shape, dtype, name=name, align_bytes=64)
+
+        l1 = tile("l1", [P, J // 16], U16)
+        l2 = tile("l2", [P, J // 16], U16)
+        l3 = tile("l3", [P, O // 16], U16)
+        l4 = tile("l4", [P, O // 16], U16)
+        l5 = tile("l5", [P, O // 16], U16)
+        xw = tile("xw", [P, T], I32)
+        xs = tile("xs", [P, T], U8)
+        ww = tile("ww", [P, 2 * R], U8)
+        w2w = tile("w2w", [P, R], I32)
+        wbw = tile("wbw", [P, N], I32)
+        ws = tile("ws", [P, R], U8)
+        w2s = tile("w2s", [P, R], U8)
+        wbs = tile("wbs", [P, N], U8)
+        slope = tile("slope", [P, 4], F32)
+        shift = tile("shift", [P, 4], F32)
+        tzt = tile("tzt", [P, 2 * E], F32)
+
+        def load_words(queue, dst, words):
+            queue.dma_start(dst[:], words[0].rearrange("p n t -> p (n t)").bitcast(I32))
+
+        def load_scales(queue, plane, scales, q):
+            rows = scales[0, 4 * q : 4 * q + 4, :].bitcast(I32)
+            queue.dma_start(plane[32 * q : 32 * q + 32, :].bitcast(I32), rows.partition_broadcast(8))
+
+        nc.sync.dma_start(l1[:], offs)
+        load_scales(nc.scalar, xs, xt_scales, 0)
+        nc.sync.dma_start(l2[:], offs2)
+        load_scales(nc.scalar, xs, xt_scales, 1)
+        load_scales(nc.sync, xs, xt_scales, 2)
+        load_scales(nc.scalar, xs, xt_scales, 3)
+        nc.sync.dma_start(ww[:].bitcast(I32), w_words[0].bitcast(I32))
+        load_words(nc.scalar, xw, xt_words)
+        for q in range(4):
+            load_scales(nc.gpsimd, w2s, w2_scales, q)
+        load_scales(nc.gpsimd, wbs, wb_scales, 3)
+        load_scales(nc.sync, ws, w_scales, 0)
+        load_words(nc.scalar, w2w, w2_words)
+        load_scales(nc.sync, ws, w_scales, 1)
+        nc.scalar.dma_start(slope[:], sg.rearrange("(p t) o -> p (t o)", t=4))
+        load_scales(nc.sync, ws, w_scales, 2)
+        nc.scalar.dma_start(shift[:], bg.rearrange("(p t) o -> p (t o)", t=4))
+        load_scales(nc.sync, ws, w_scales, 3)
+        nc.scalar.dma_start(tzt[:].rearrange("p (h e) -> p h e", h=2), tz.rearrange("(h p) e -> p h e", h=2))
+        nc.sync.dma_start(l3[:], offs3)
+        nc.sync.dma_start(l4[:], offs4)
+        nc.sync.dma_start(l5[:], offs5)
+        load_words(nc.sync, wbw, wb_words)
+        for q in range(3):
+            load_scales(nc.sync, wbs, wb_scales, q)
+
+        gs1 = tile("gs1", [P, J], U8)
+        gs2 = tile("gs2", [P, J], U8)
+        gw1 = tile("gw1", [P, J], U32)
+        gw2 = tile("gw2", [P, J], U32)
+        wwp = tile("wwp", [P, 2 * R], U8)
+        wsp = tile("wsp", [P, R], U8)
+        w2wp = tile("w2wp", [P, R], U32)
+        w2sp = tile("w2sp", [P, R], U8)
+
+        def deal(engine_copy, dst, src):
+            engine_copy(dst.rearrange("p (t m) -> p t m", t=4), src.rearrange("p (m t) -> p t m", t=4))
+
+        nc.vector.tensor_copy(gs1[:], xs[:].indirect(l1[:]))
+        nc.vector.tensor_copy(gs2[:], xs[:].indirect(l2[:]))
+        deal(nc.vector.tensor_copy, wwp[:].bitcast(U16), ww[:].bitcast(U16))
+        deal(nc.vector.tensor_copy, wsp[:], ws[:])
+        deal(nc.vector.tensor_copy, w2sp[:], w2s[:])
+        nc.vector.tensor_copy(gw1[:], xw[:].bitcast(U32).indirect(l1[:]))
+        nc.vector.tensor_copy(gw2[:], xw[:].bitcast(U32).indirect(l2[:]))
+        deal(nc.scalar.copy, w2wp[:], w2w[:].bitcast(U32))
+
+        pa = [ps.tile([P, J], F32, name="pa%d" % t, tag="pa%d" % t) for t in range(4)]
+        pb = [ps.tile([P, J], F32, name="pb%d" % t) for t in range(4)]
+        for t in range(4):
+            nc.tensor.matmul_mx(
+                out=pa[t][:], lhsT=wwp[:, 2 * P * t : 2 * P * (t + 1)].bitcast(E2M1), lhsT_scale=wsp[:, P * t : P * (t + 1)],
+                rhs=gw1[:].bitcast(E4M3), rhs_scale=gs1[:], start=True, stop=True,
+            )
+        for t in range(4):
+            nc.tensor.matmul_mx(
+                out=pb[t][:], lhsT=w2wp[:, P * t : P * (t + 1)].bitcast(E5M2), lhsT_scale=w2sp[:, P * t : P * (t + 1)],
+                rhs=gw2[:].bitcast(E4M3), rhs_scale=gs2[:], start=True, stop=True,
+            )
+
+        at = [tile("a%d" % t, [P, J], F32) for t in range(4)]
+        bt = [tile("b%d" % t, [P, J], F32) for t in range(4)]
+        gate = tile("gate", [P, 4, O], F32)
+        bsel = tile("bsel", [P, 4, O], F32)
+        for t in range(4):
+            if t == 0:
+                nc.scalar.copy(at[t][:], pa[t][:])
+            else:
+                nc.vector.tensor_copy(at[t][:], pa[t][:])
+            nc.scalar.activation(
+                out=gate[:, t, :], in_=at[t][:].indirect(l3[:]), func=ACT.Sigmoid,
+                bias=shift[:, t : t + 1], scale=slope[:, t : t + 1],
+            )
+        for t in range(4):
+            if t % 2 == 0:
+                nc.vector.tensor_copy(bt[t][:], pb[t][:])
+            else:
+                nc.scalar.copy(bt[t][:], pb[t][:])
+        for t in range(4):
+            if t < 3:
+                nc.vector.tensor_copy(bsel[:, t, :], bt[t][:].indirect(l4[:]))
+            else:
+                nc.scalar.activation(out=bsel[:, t, :], in_=bt[t][:].indirect(l4[:]), func=ACT.Copy)
+
+        tsel = tile("tsel", [P, 2, O], F32)
+        for h in range(2):
+            nc.scalar.activation(out=tsel[:, h, :], in_=tzt[:, h * E : (h + 1) * E].indirect(l5[:]), func=ACT.Copy)
+
+        hid = tile("hid", [P, O, 4], BF16)
+        hw = tile("hw", [P, O], U32)
+        hs = tile("hs", [P, O], U8)
+        nc.vector.tensor_tensor(hid[:], bsel[:].rearrange("p t o -> p o t"), gate[:].rearrange("p t o -> p o t"), ALU.mult)
+        nc.vector.quantize_mx(out=hw[:].bitcast(E4M3), scales=hs[:], in_=hid[:].rearrange("p o t -> p (o t)"))
+        pp = ps.tile([P, 2, O], F32, name="pp", tag="pa0")
+        for h in range(2):
+            nc.tensor.matmul_mx(
+                out=pp[:, h, :], lhsT=wbw[:, P * h : P * (h + 1)].bitcast(E5M2), lhsT_scale=wbs[:, P * h : P * (h + 1)],
+                rhs=hw[:].bitcast(E4M3), rhs_scale=hs[:], start=True, stop=True,
+            )
+        res = tile("res", [P, 2, O], F32)
+        nc.vector.tensor_tensor(res[:], pp[:], tsel[:], ALU.add)
+        nc.sync.dma_start(out.rearrange("(h p) o -> p h o", h=2), res[:])

@@ -28,8 +28,8 @@ def tile_list_ahead_gatefetch_one_tabled_kernel(
         sb = ctx.enter_context(tc.tile_pool(name="sb", bufs=1))
         ps = ctx.enter_context(tc.psum_pool(name="ps", bufs=1))
 
-        def tile(name, shape, dtype):
-            return sb.tile(shape, dtype, name=name, align_bytes=64)
+        def tile(name, shape, dtype, tag=""):
+            return sb.tile(shape, dtype, name=name, tag=tag or name, align_bytes=64)
 
         l1 = tile("l1", [P, J // 16], U16)
         l2 = tile("l2", [P, J // 16], U16)
@@ -57,28 +57,32 @@ def tile_list_ahead_gatefetch_one_tabled_kernel(
 
         nc.sync.dma_start(l1[:], offs)
         load_scales(nc.scalar, xs, xt_scales, 0)
-        nc.sync.dma_start(l2[:], offs2)
+        nc.sync.dma_start(ww[:].bitcast(I32), w_words[0].bitcast(I32))
         load_scales(nc.scalar, xs, xt_scales, 1)
         load_scales(nc.sync, xs, xt_scales, 2)
         load_scales(nc.scalar, xs, xt_scales, 3)
-        nc.sync.dma_start(ww[:].bitcast(I32), w_words[0].bitcast(I32))
+        nc.sync.dma_start(l2[:], offs2)
         load_words(nc.scalar, xw, xt_words)
-        for q in range(4):
-            load_scales(nc.gpsimd, w2s, w2_scales, q)
-        load_scales(nc.gpsimd, wbs, wb_scales, 3)
+        load_scales(nc.gpsimd, ws, w_scales, 3)
+        load_scales(nc.gpsimd, w2s, w2_scales, 3)
+        nc.gpsimd.dma_start(shift[:], bg.rearrange("(p t) o -> p (t o)", t=4))
         load_scales(nc.sync, ws, w_scales, 0)
         load_words(nc.scalar, w2w, w2_words)
-        load_scales(nc.sync, ws, w_scales, 1)
-        nc.scalar.dma_start(slope[:], sg.rearrange("(p t) o -> p (t o)", t=4))
-        load_scales(nc.sync, ws, w_scales, 2)
-        nc.scalar.dma_start(shift[:], bg.rearrange("(p t) o -> p (t o)", t=4))
-        load_scales(nc.sync, ws, w_scales, 3)
-        nc.scalar.dma_start(tzt[:].rearrange("p (h e) -> p h e", h=2), tz.rearrange("(h p) e -> p h e", h=2))
+        warm = tile("warm", [P, 1], F32)
+        warm_in = tile("warm_in", [P, 1], F32)
+        nc.vector.memset(warm_in[:], 0.0)
+        nc.scalar.activation(out=warm[:], in_=warm_in[:], func=ACT.Sigmoid)
+        for q in (1, 2):
+            load_scales(nc.sync, ws, w_scales, q)
+        for q in range(3):
+            load_scales(nc.sync, w2s, w2_scales, q)
         nc.sync.dma_start(l3[:], offs3)
+        nc.sync.dma_start(slope[:], sg.rearrange("(p t) o -> p (t o)", t=4))
         nc.sync.dma_start(l4[:], offs4)
+        nc.sync.dma_start(tzt[:].rearrange("p (h e) -> p h e", h=2), tz.rearrange("(h p) e -> p h e", h=2))
         nc.sync.dma_start(l5[:], offs5)
         load_words(nc.sync, wbw, wb_words)
-        for q in range(3):
+        for q in range(4):
             load_scales(nc.sync, wbs, wb_scales, q)
 
         gs1 = tile("gs1", [P, J], U8)
@@ -94,13 +98,13 @@ def tile_list_ahead_gatefetch_one_tabled_kernel(
             engine_copy(dst.rearrange("p (t m) -> p t m", t=4), src.rearrange("p (m t) -> p t m", t=4))
 
         nc.vector.tensor_copy(gs1[:], xs[:].indirect(l1[:]))
-        nc.vector.tensor_copy(gs2[:], xs[:].indirect(l2[:]))
         deal(nc.vector.tensor_copy, wwp[:].bitcast(U16), ww[:].bitcast(U16))
+        nc.vector.tensor_copy(gs2[:], xs[:].indirect(l2[:]))
         deal(nc.vector.tensor_copy, wsp[:], ws[:])
-        deal(nc.vector.tensor_copy, w2sp[:], w2s[:])
         nc.vector.tensor_copy(gw1[:], xw[:].bitcast(U32).indirect(l1[:]))
         nc.vector.tensor_copy(gw2[:], xw[:].bitcast(U32).indirect(l2[:]))
-        deal(nc.scalar.copy, w2wp[:], w2w[:].bitcast(U32))
+        deal(nc.vector.tensor_copy, w2sp[:], w2s[:])
+        nc.scalar.copy(w2wp[:].rearrange("p (t m) -> p m t", t=4), w2w[:].bitcast(U32).rearrange("p (m t) -> p m t", t=4))
 
         pa = [ps.tile([P, J], F32, name="pa%d" % t, tag="pa%d" % t) for t in range(4)]
         pb = [ps.tile([P, J], F32, name="pb%d" % t) for t in range(4)]
@@ -119,41 +123,41 @@ def tile_list_ahead_gatefetch_one_tabled_kernel(
         bt = [tile("b%d" % t, [P, J], F32) for t in range(4)]
         gate = tile("gate", [P, 4, O], F32)
         bsel = tile("bsel", [P, 4, O], F32)
-        for t in range(4):
-            if t == 0:
-                nc.scalar.copy(at[t][:], pa[t][:])
-            else:
-                nc.vector.tensor_copy(at[t][:], pa[t][:])
-            nc.scalar.activation(
-                out=gate[:, t, :], in_=at[t][:].indirect(l3[:]), func=ACT.Sigmoid,
-                bias=shift[:, t : t + 1], scale=slope[:, t : t + 1],
-            )
-        for t in range(4):
-            if t % 2 == 0:
-                nc.vector.tensor_copy(bt[t][:], pb[t][:])
-            else:
-                nc.scalar.copy(bt[t][:], pb[t][:])
-        for t in range(4):
-            if t < 3:
-                nc.vector.tensor_copy(bsel[:, t, :], bt[t][:].indirect(l4[:]))
-            else:
-                nc.scalar.activation(out=bsel[:, t, :], in_=bt[t][:].indirect(l4[:]), func=ACT.Copy)
+        nc.scalar.copy(at[0][:], pa[0][:])
+        nc.scalar.copy(at[1][:], pa[1][:])
+        nc.scalar.copy(at[2][:], pa[2][:])
+        nc.scalar.copy(at[3][:], pa[3][:])
+        nc.scalar.copy(bt[0][:], pb[0][:])
+        nc.scalar.activation(out=gate[:, 0, :], in_=at[0][:].indirect(l3[:]), func=ACT.Sigmoid, bias=shift[:, 0 : 1], scale=slope[:, 0 : 1])
+        nc.scalar.activation(out=gate[:, 1, :], in_=at[1][:].indirect(l3[:]), func=ACT.Sigmoid, bias=shift[:, 1 : 2], scale=slope[:, 1 : 2])
+        nc.scalar.activation(out=gate[:, 2, :], in_=at[2][:].indirect(l3[:]), func=ACT.Sigmoid, bias=shift[:, 2 : 3], scale=slope[:, 2 : 3])
+        nc.scalar.activation(out=gate[:, 3, :], in_=at[3][:].indirect(l3[:]), func=ACT.Sigmoid, bias=shift[:, 3 : 4], scale=slope[:, 3 : 4])
+        nc.vector.tensor_copy(bt[1][:], pb[1][:])
+        nc.vector.tensor_copy(bt[2][:], pb[2][:])
+        nc.vector.tensor_copy(bt[3][:], pb[3][:])
+        nc.vector.tensor_copy(bsel[:, 0, :], bt[0][:].indirect(l4[:]))
+        nc.vector.tensor_copy(bsel[:, 1, :], bt[1][:].indirect(l4[:]))
+        nc.vector.tensor_copy(bsel[:, 2, :], bt[2][:].indirect(l4[:]))
+        nc.vector.tensor_copy(bsel[:, 3, :], bt[3][:].indirect(l4[:]))
 
-        tsel = tile("tsel", [P, 2, O], F32)
+        tsel = tile("tsel", [P, 2, O], F32, tag="a3")
         for h in range(2):
             nc.scalar.activation(out=tsel[:, h, :], in_=tzt[:, h * E : (h + 1) * E].indirect(l5[:]), func=ACT.Copy)
 
         hid = tile("hid", [P, O, 4], BF16)
         hw = tile("hw", [P, O], U32)
         hs = tile("hs", [P, O], U8)
-        nc.vector.tensor_tensor(hid[:], bsel[:].rearrange("p t o -> p o t"), gate[:].rearrange("p t o -> p o t"), ALU.mult)
-        nc.vector.quantize_mx(out=hw[:].bitcast(E4M3), scales=hs[:], in_=hid[:].rearrange("p o t -> p (o t)"))
-        pp = ps.tile([P, 2, O], F32, name="pp", tag="pa0")
-        for h in range(2):
+        halves = (slice(0, O // 2), slice(O // 2, O))
+        for cols in halves:
+            nc.vector.tensor_tensor(hid[:, cols, :], bsel[:, :, cols].rearrange("p t o -> p o t"), gate[:, :, cols].rearrange("p t o -> p o t"), ALU.mult)
+        for cols in halves:
+            nc.vector.quantize_mx(out=hw[:, cols].bitcast(E4M3), scales=hs[:, cols], in_=hid[:, cols, :].rearrange("p o t -> p (o t)"))
+        res = [tile("res%d" % h, [P, O], F32) for h in range(2)]
+        for h, queue in enumerate((nc.sync, nc.scalar)):
+            pp = ps.tile([P, O], F32, name="pp%d" % h, tag="pa%d" % h)
             nc.tensor.matmul_mx(
-                out=pp[:, h, :], lhsT=wbw[:, P * h : P * (h + 1)].bitcast(E5M2), lhsT_scale=wbs[:, P * h : P * (h + 1)],
+                out=pp[:], lhsT=wbw[:, P * h : P * (h + 1)].bitcast(E5M2), lhsT_scale=wbs[:, P * h : P * (h + 1)],
                 rhs=hw[:].bitcast(E4M3), rhs_scale=hs[:], start=True, stop=True,
             )
-        res = tile("res", [P, 2, O], F32)
-        nc.vector.tensor_tensor(res[:], pp[:], tsel[:], ALU.add)
-        nc.sync.dma_start(out.rearrange("(h p) o -> p h o", h=2), res[:])
+            nc.vector.tensor_tensor(res[h][:], pp[:], tsel[:, h, :], ALU.add)
+            queue.dma_start(out[h * P : (h + 1) * P, :], res[h][:])

@@ -119,13 +119,13 @@ def tile_list_ahead_gatefetch_one_tabled_kernel(
                 rhs=gw2[:].bitcast(E4M3), rhs_scale=gs2[:], start=True, stop=True,
             )
 
-        at = [tile("a%d" % t, [P, J], F32) for t in range(4)]
+        at = [tile("a%d" % t, [P, J], F32, tag="w2s" if t == 2 else "") for t in range(4)]
         bt = [tile("b%d" % t, [P, J], F32) for t in range(4)]
         gate = tile("gate", [P, 4, O], F32)
         bsel = tile("bsel", [P, 4, O], F32)
         nc.scalar.copy(at[0][:], pa[0][:])
         nc.scalar.copy(at[1][:], pa[1][:])
-        nc.scalar.copy(at[2][:], pa[2][:])
+        nc.vector.tensor_copy(at[2][:], pa[2][:])
         nc.scalar.copy(at[3][:], pa[3][:])
         nc.scalar.copy(bt[0][:], pb[0][:])
         nc.scalar.activation(out=gate[:, 0, :], in_=at[0][:].indirect(l3[:]), func=ACT.Sigmoid, bias=shift[:, 0 : 1], scale=slope[:, 0 : 1])
@@ -138,9 +138,9 @@ def tile_list_ahead_gatefetch_one_tabled_kernel(
         nc.vector.tensor_copy(bsel[:, 0, :], bt[0][:].indirect(l4[:]))
         nc.vector.tensor_copy(bsel[:, 1, :], bt[1][:].indirect(l4[:]))
         nc.vector.tensor_copy(bsel[:, 2, :], bt[2][:].indirect(l4[:]))
-        nc.vector.tensor_copy(bsel[:, 3, :], bt[3][:].indirect(l4[:]))
+        nc.scalar.activation(out=bsel[:, 3, :], in_=bt[3][:].indirect(l4[:]), func=ACT.Copy)
 
-        tsel = tile("tsel", [P, 2, O], F32, tag="a3")
+        tsel = tile("tsel", [P, 2, O], F32, tag="b3")
         for h in range(2):
             nc.scalar.activation(out=tsel[:, h, :], in_=tzt[:, h * E : (h + 1) * E].indirect(l5[:]), func=ACT.Copy)
 
@@ -149,7 +149,12 @@ def tile_list_ahead_gatefetch_one_tabled_kernel(
         hs = tile("hs", [P, O], U8)
         halves = (slice(0, O // 2), slice(O // 2, O))
         for cols in halves:
-            nc.vector.tensor_tensor(hid[:, cols, :], bsel[:, :, cols].rearrange("p t o -> p o t"), gate[:, :, cols].rearrange("p t o -> p o t"), ALU.mult)
+            nc.vector.tensor_tensor(
+                hid[:, cols, :].rearrange("p (c i) t -> p c t i", i=4),
+                bsel[:, :, cols].rearrange("p t (c i) -> p c t i", i=4),
+                gate[:, :, cols].rearrange("p t (c i) -> p c t i", i=4),
+                ALU.mult,
+            )
         for cols in halves:
             nc.vector.quantize_mx(out=hw[:, cols].bitcast(E4M3), scales=hs[:, cols], in_=hid[:, cols, :].rearrange("p o t -> p (o t)"))
         res = [tile("res%d" % h, [P, O], F32) for h in range(2)]

from contextlib import ExitStack

import concourse.mybir as mybir

K, T, J, R, O, N, E = 512, 2048, 256, 512, 128, 256, 1024
FLOPS = 2 * K * R * J * 2 + 2 * R * N * O

F32 = mybir.dt.float32
BF16 = mybir.dt.bfloat16
I32 = mybir.dt.int32
U32 = mybir.dt.uint32
U16 = mybir.dt.uint16
U8 = mybir.dt.uint8
E4M3 = mybir.dt.float8_e4m3fn_x4
E5M2 = mybir.dt.float8_e5m2_x4
E2M1 = mybir.dt.float4_e2m1fn_x4
ACT = mybir.ActivationFunctionType
ALU = mybir.AluOpType
P = 128


def tile_list_ahead_gatefetch_one_tabled_kernel(
    tc, xt_words, xt_scales, w_words, w_scales, w2_words, w2_scales, sg, bg,
    wb_words, wb_scales, tz, offs, offs2, offs3, offs4, offs5, out,
):
    nc = tc.nc
    with ExitStack() as ctx:
        sb = ctx.enter_context(tc.tile_pool(name="sb", bufs=1))
        ps = ctx.enter_context(tc.psum_pool(name="ps", bufs=1))

        def tile(name, shape, dtype, tag=""):
            return sb.tile(shape, dtype, name=name, tag=tag or name, align_bytes=64)

        l1 = tile("l1", [P, J // 16], U16)
        l2 = tile("l2", [P, J // 16], U16)
        l3 = tile("l3", [P, O // 16], U16)
        l4 = tile("l4", [P, O // 16], U16)
        l5 = tile("l5", [P, O // 16], U16)
        xw = tile("xw", [P, T], I32)
        xs = tile("xs", [P, T], U8)
        ww = tile("ww", [P, 2 * R], U8)
        w2w = tile("w2w", [P, R], I32)
        wbw = tile("wbw", [P, N], I32)
        ws = tile("ws", [P, R], U8)
        w2s = tile("w2s", [P, R], U8)
        wbs = tile("wbs", [P, N], U8)
        slope = tile("slope", [P, 4], F32)
        shift = tile("shift", [P, 4], F32)
        tzt = tile("tzt", [P, 2 * E], F32)

        def load_words(queue, dst, words):
            queue.dma_start(dst[:], words[0].rearrange("p n t -> p (n t)").bitcast(I32))

        def load_scales(queue, plane, scales, q):
            rows = scales[0, 4 * q : 4 * q + 4, :].bitcast(I32)
            queue.dma_start(plane[32 * q : 32 * q + 32, :].bitcast(I32), rows.partition_broadcast(8))

        nc.sync.dma_start(l1[:], offs)
        load_scales(nc.scalar, xs, xt_scales, 0)
        nc.sync.dma_start(ww[:].bitcast(I32), w_words[0].bitcast(I32))
        load_scales(nc.scalar, xs, xt_scales, 1)
        load_scales(nc.sync, xs, xt_scales, 2)
        load_scales(nc.scalar, xs, xt_scales, 3)
        nc.sync.dma_start(l2[:], offs2)
        load_words(nc.scalar, xw, xt_words)
        load_scales(nc.gpsimd, ws, w_scales, 3)
        load_scales(nc.gpsimd, w2s, w2_scales, 3)
        nc.gpsimd.dma_start(shift[:], bg.rearrange("(p t) o -> p (t o)", t=4))
        load_scales(nc.sync, ws, w_scales, 0)
        load_words(nc.scalar, w2w, w2_words)
        warm = tile("warm", [P, 1], F32)
        warm_in = tile("warm_in", [P, 1], F32)
        nc.vector.memset(warm_in[:], 0.0)
        nc.scalar.activation(out=warm[:], in_=warm_in[:], func=ACT.Sigmoid)
        for q in (1, 2):
            load_scales(nc.sync, ws, w_scales, q)
        for q in range(3):
            load_scales(nc.sync, w2s, w2_scales, q)
        nc.sync.dma_start(l3[:], offs3)
        nc.sync.dma_start(slope[:], sg.rearrange("(p t) o -> p (t o)", t=4))
        nc.sync.dma_start(l4[:], offs4)
        nc.sync.dma_start(tzt[:].rearrange("p (h e) -> p h e", h=2), tz.rearrange("(h p) e -> p h e", h=2))
        nc.sync.dma_start(l5[:], offs5)
        load_words(nc.sync, wbw, wb_words)
        for q in range(4):
            load_scales(nc.sync, wbs, wb_scales, q)

        gs1 = tile("gs1", [P, J], U8)
        gs2 = tile("gs2", [P, J], U8)
        gw1 = tile("gw1", [P, J], U32)
        gw2 = tile("gw2", [P, J], U32)
        wwp = tile("wwp", [P, 2 * R], U8)
        wsp = tile("wsp", [P, R], U8)
        w2wp = tile("w2wp", [P, R], U32)
        w2sp = tile("w2sp", [P, R], U8)

        def deal(engine_copy, dst, src):
            engine_copy(dst.rearrange("p (t m) -> p t m", t=4), src.rearrange("p (m t) -> p t m", t=4))

        nc.vector.tensor_copy(gs1[:], xs[:].indirect(l1[:]))
        deal(nc.vector.tensor_copy, wwp[:].bitcast(U16), ww[:].bitcast(U16))
        nc.vector.tensor_copy(gs2[:], xs[:].indirect(l2[:]))
        deal(nc.vector.tensor_copy, wsp[:], ws[:])
        nc.vector.tensor_copy(gw1[:], xw[:].bitcast(U32).indirect(l1[:]))
        nc.vector.tensor_copy(gw2[:], xw[:].bitcast(U32).indirect(l2[:]))
        deal(nc.vector.tensor_copy, w2sp[:], w2s[:])
        nc.scalar.copy(w2wp[:].rearrange("p (t m) -> p m t", t=4), w2w[:].bitcast(U32).rearrange("p (m t) -> p m t", t=4))

        pa = [ps.tile([P, J], F32, name="pa%d" % t, tag="pa%d" % t) for t in range(4)]
        pb = [ps.tile([P, J], F32, name="pb%d" % t) for t in range(4)]
        for t in range(4):
            nc.tensor.matmul_mx(
                out=pa[t][:], lhsT=wwp[:, 2 * P * t : 2 * P * (t + 1)].bitcast(E2M1), lhsT_scale=wsp[:, P * t : P * (t + 1)],
                rhs=gw1[:].bitcast(E4M3), rhs_scale=gs1[:], start=True, stop=True,
            )
        for t in range(4):
            nc.tensor.matmul_mx(
                out=pb[t][:], lhsT=w2wp[:, P * t : P * (t + 1)].bitcast(E5M2), lhsT_scale=w2sp[:, P * t : P * (t + 1)],
                rhs=gw2[:].bitcast(E4M3), rhs_scale=gs2[:], start=True, stop=True,
            )

        at = [tile("a%d" % t, [P, J], F32, tag="w2s" if t == 2 else "") for t in range(4)]
        bt = [tile("b%d" % t, [P, J], F32) for t in range(4)]
        gate = tile("gate", [P, 4, O], F32)
        bsel = tile("bsel", [P, 4, O], F32)
        nc.scalar.copy(at[0][:], pa[0][:])
        nc.scalar.copy(at[1][:], pa[1][:])
        nc.vector.tensor_copy(at[2][:], pa[2][:])
        nc.scalar.copy(at[3][:], pa[3][:])
        nc.scalar.copy(bt[0][:], pb[0][:])
        nc.scalar.activation(out=gate[:, 0, :], in_=at[0][:].indirect(l3[:]), func=ACT.Sigmoid, bias=shift[:, 0 : 1], scale=slope[:, 0 : 1])
        nc.scalar.activation(out=gate[:, 1, :], in_=at[1][:].indirect(l3[:]), func=ACT.Sigmoid, bias=shift[:, 1 : 2], scale=slope[:, 1 : 2])
        nc.scalar.activation(out=gate[:, 2, :], in_=at[2][:].indirect(l3[:]), func=ACT.Sigmoid, bias=shift[:, 2 : 3], scale=slope[:, 2 : 3])
        nc.scalar.activation(out=gate[:, 3, :], in_=at[3][:].indirect(l3[:]), func=ACT.Sigmoid, bias=shift[:, 3 : 4], scale=slope[:, 3 : 4])
        nc.vector.tensor_copy(bt[1][:], pb[1][:])
        nc.vector.tensor_copy(bt[2][:], pb[2][:])
        nc.vector.tensor_copy(bt[3][:], pb[3][:])
        nc.vector.tensor_copy(bsel[:, 0, :], bt[0][:].indirect(l4[:]))
        nc.vector.tensor_copy(bsel[:, 1, :], bt[1][:].indirect(l4[:]))
        nc.vector.tensor_copy(bsel[:, 2, :], bt[2][:].indirect(l4[:]))
        nc.scalar.activation(out=bsel[:, 3, :], in_=bt[3][:].indirect(l4[:]), func=ACT.Copy)

        tsel = tile("tsel", [P, 2, O], F32, tag="b3")
        for h in range(2):
            nc.scalar.activation(out=tsel[:, h, :], in_=tzt[:, h * E : (h + 1) * E].indirect(l5[:]), func=ACT.Copy)

        hid = tile("hid", [P, O, 4], BF16)
        hw = tile("hw", [P, O], U32)
        hs = tile("hs", [P, O], U8)
        halves = (slice(0, O // 2), slice(O // 2, O))
        for cols in halves:
            nc.vector.tensor_tensor(
                hid[:, cols, :].rearrange("p (c i) t -> p c t i", i=4),
                bsel[:, :, cols].rearrange("p t (c i) -> p c t i", i=4),
                gate[:, :, cols].rearrange("p t (c i) -> p c t i", i=4),
                ALU.mult,
            )
        for cols in halves:
            nc.vector.quantize_mx(out=hw[:, cols].bitcast(E4M3), scales=hs[:, cols], in_=hid[:, cols, :].rearrange("p o t -> p (o t)"))
        res = [tile("res%d" % h, [P, O], F32) for h in range(2)]
        for h, queue in enumerate((nc.sync, nc.scalar)):
            pp = ps.tile([P, O], F32, name="pp%d" % h, tag="pa%d" % h)
            nc.tensor.matmul_mx(
                out=pp[:], lhsT=wbw[:, P * h : P * (h + 1)].bitcast(E5M2), lhsT_scale=wbs[:, P * h : P * (h + 1)],
                rhs=hw[:].bitcast(E4M3), rhs_scale=hs[:], start=True, stop=True,
            )
            nc.vector.tensor_tensor(res[h][:], pp[:], tsel[:, h, :], ALU.add)
            queue.dma_start(out[h * P : (h + 1) * P, :], res[h][:])
